import numpy as np
import ml_dtypes


def mxq(x, axis, fmt="e4m3"):
    dtype, down = {"e4m3": (ml_dtypes.float8_e4m3fn, 7), "e5m2": (ml_dtypes.float8_e5m2, 14)}[fmt]
    v = np.moveaxis(np.asarray(x, np.float32).astype(ml_dtypes.bfloat16).astype(np.float64), axis, -1)
    blocks = v.reshape(v.shape[:-1] + (-1, 32))
    amax = np.abs(blocks).max(-1, keepdims=True)
    byte = np.maximum(np.where(amax > 0, np.frexp(amax)[1] - 1 + 127, 0) - down, 1)
    scale = np.exp2(byte - 127.0)
    codes = (blocks / scale).astype(np.float32).astype(dtype).astype(np.float64)
    return np.moveaxis((codes * scale).reshape(v.shape), -1, axis)


WIDE = False


def mx_kscale(k):
    if not WIDE:
        return np.ones(k)
    levels = np.array([10, -10, 5, -5, 0])
    if k % 512:
        return np.exp2(np.random.permutation(np.resize(levels, k // 32))).repeat(32)
    a = np.empty((k // 512, 16))
    for p in range(k // 512):
        a[p, :8] = np.random.permutation(np.resize(levels, 8))
        for g in range(8):
            far = levels[np.abs(levels - a[p, g]) >= 10]
            a[p, g + 8] = far[np.random.randint(len(far))]
    return np.exp2(a.ravel()).repeat(32)


def f64(x):
    return np.asarray(x).astype(np.float64)


def striped(idx):
    return np.tile(np.asarray(idx).reshape(-1, 16).T, (8, 1)).astype(np.uint16)


def unstriped(offs):
    return offs[:16].T.reshape(-1).astype(np.int64)


B, N, C, D, NQ = 1, 1024, 2048, 1024, 128


def eight(codes):
    return np.concatenate([codes[h].reshape(-1, 16).T for h in range(8)]).astype(np.uint16)


def uneight(offs):
    return np.stack([offs[16 * h:16 * h + 16].T.reshape(-1) for h in range(8)]).astype(np.int64)


def setup_inputs():
    n = np.random.standard_normal
    s = mx_kscale(D)[:, None]
    grid = lambda x: np.round(x * 32) / 32
    return {
        "qT": (n((B, D, NQ)) * s / np.sqrt(D)).astype(np.float32),
        "cb": (grid(n((D, C))) / s).astype(np.float32),
        "norm": np.tile(np.random.randint(32, 129, N) / 64.0, (128, 1)).astype(np.float32),
        "bias": np.tile(n(N), (128, 1)).astype(np.float32),
        "offs": eight(np.random.randint(0, C, (8, N))),
        "offs2": eight(np.random.randint(0, C, (8, N))),
    }


def reference(qT, cb, norm, bias, offs, offs2):
    k = []
    for part, offs_ in enumerate((offs, offs2,)):
        codes = uneight(offs_)
        k += [f64(cb)[512 * part + 64 * h:512 * part + 64 * h + 64][:, codes[h]] for h in range(8)]
    k = np.concatenate(k) * f64(norm)[:1]
    a = mxq(f64(qT), 1, "e4m3").transpose(0, 2, 1) @ mxq(k, 0, "e4m3")
    a = a + f64(bias)[:1]
    return a

@@ -1,0 +1,151 @@
+import concourse.mybir as mybir
+from concourse.masks import make_identity
+
+NQ, D, N, C = 128, 1024, 1024, 2048
+FLOPS = 2 * NQ * D * N
+
+F32 = mybir.dt.float32
+BF16 = mybir.dt.bfloat16
+U32 = mybir.dt.uint32
+U16 = mybir.dt.uint16
+U8 = mybir.dt.uint8
+FP8X4 = mybir.dt.float8_e4m3fn_x4
+MULT = mybir.AluOpType.mult
+ADD = mybir.AluOpType.add
+
+P = 128
+PACK = 4
+PASSES = D // (P * PACK)
+LIST = 16
+HALF = N // 2
+RUN = N // P
+
+PIECES = [(0, 512), (512, 256), (768, 128), (896, 128)]
+
+
+def tile_attend_pq_lin_bias_kernel(tc, qT, cb, norm, bias, offs, offs2, out):
+    nc = tc.nc
+    cb_planes = cb.rearrange("(g p t) c -> g t p c", g=PASSES, t=PACK)
+    q_rows = qT[0].rearrange("(g p t) q -> p g t q", g=PASSES, t=PACK)
+
+    with (
+        tc.tile_pool(name="keep", bufs=1) as keep,
+        tc.psum_pool(name="psum", bufs=1) as psum,
+    ):
+        lists = [keep.tile([P, N // LIST], U16, name=f"list{g}") for g in range(PASSES)]
+        norm_runs = keep.tile([P, RUN], F32, name="norm_runs")
+        identity = keep.tile([P, P], F32, name="identity")
+        norm_sb = keep.tile([P, N], F32, name="norm_sb")
+        bias_sb = keep.tile([P, N], F32, name="bias_sb")
+        planes = [[keep.tile([P, C], F32, name=f"plane{g}{t}") for t in range(PACK)] for g in range(PASSES)]
+        q_raw = keep.tile([P, PASSES, PACK, NQ], F32, name="q_raw")
+        q_grouped = keep.tile([P, PASSES, NQ, PACK], BF16, name="q_grouped", align_bytes=64)
+        q_codes = keep.tile([P, PASSES * NQ], U32, name="q_codes", align_bytes=64)
+        q_scales = keep.tile([P, PASSES * NQ], U8, name="q_scales", align_bytes=64)
+        k_raw = [keep.tile([P, PACK, N], F32, name=f"k_raw{g}") for g in range(PASSES)]
+        k_grouped = [keep.tile([P, N, PACK], BF16, name=f"k_grouped{g}", align_bytes=64) for g in range(PASSES)]
+        k_codes = [keep.tile([P, N], U32, name=f"k_codes{g}", align_bytes=64) for g in range(PASSES)]
+        k_scales = [keep.tile([P, N], U8, name=f"k_scales{g}", align_bytes=64) for g in range(PASSES)]
+        out_sb = keep.tile([P, N], F32, name="out_sb")
+        banks = [psum.tile([P, width], F32, name=f"bank{i}") for i, (start, width) in enumerate(PIECES)]
+        spread = [psum.tile([P, PACK, P], F32, name=f"spread{e}") for e in range(RUN // PACK)]
+
+        nc.scalar.dma_start(norm_runs[:], norm[0].rearrange("(p j) -> p j", j=RUN))
+        nc.sync.dma_start(lists[0][:], offs)
+        for t in range(PACK):
+            nc.sync.dma_start(planes[0][t][:], cb_planes[0, t])
+        nc.sync.dma_start(lists[1][:], offs2)
+        nc.sync.dma_start(planes[1][0][:], cb_planes[1, 0])
+        nc.sync.dma_start(planes[1][1][:], cb_planes[1, 1])
+        nc.sync.dma_start(q_raw[:], q_rows)
+        nc.sync.dma_start(planes[1][2][:], cb_planes[1, 2])
+        nc.sync.dma_start(planes[1][3][:], cb_planes[1, 3])
+        nc.sync.dma_start(bias_sb[:], bias)
+
+        make_identity(nc, identity[:])
+        for j in range(RUN):
+            nc.tensor.transpose(
+                spread[j // PACK][:, j % PACK, :], norm_runs[:, j : j + 1].to_broadcast([P, P]), identity[:]
+            )
+        norm_view = norm_sb[:].rearrange("p (n e j) -> p e n j", e=RUN // PACK, j=PACK)
+        for part in (slice(0, P // 2), slice(P // 2, P)):
+            for e, copy in ((0, nc.vector.tensor_copy), (1, nc.scalar.copy)):
+                copy(norm_view[:, e, part, :], spread[e][:, :, part].rearrange("p j n -> p n j"))
+
+        def gather(g, t, start, width):
+            cols = slice(start, start + width)
+            entries = lists[g][:, start // LIST : (start + width) // LIST]
+            nc.vector.tensor_tensor(k_raw[g][:, t, cols], planes[g][t][:].indirect(entries), norm_sb[:, cols], MULT)
+
+        def interleave(g, start, width):
+            cols = slice(start, start + width)
+            nc.scalar.copy(
+                k_grouped[g][:, cols, :].rearrange("p (c i) t -> p c t i", i=4),
+                k_raw[g][:, :, cols].rearrange("p t (c i) -> p c t i", i=4),
+            )
+
+        def quantise(g, start, width):
+            cols = slice(start, start + width)
+            nc.vector.quantize_mx(
+                out=k_codes[g][:, cols].bitcast(FP8X4),
+                scales=k_scales[g][:, cols],
+                in_=k_grouped[g][:, cols, :].rearrange("p c t -> p (c t)"),
+            )
+
+        def multiply(g, i):
+            start, width = PIECES[i]
+            cols = slice(start, start + width)
+            rows = slice(g * NQ, (g + 1) * NQ)
+            nc.tensor.matmul_mx(
+                out=banks[i][:],
+                lhsT=q_codes[:, rows].bitcast(FP8X4),
+                lhsT_scale=q_scales[:, rows],
+                rhs=k_codes[g][:, cols].bitcast(FP8X4),
+                rhs_scale=k_scales[g][:, cols],
+                start=(g == 0),
+                stop=(g == PASSES - 1),
+            )
+
+        def finish(i):
+            start, width = PIECES[i]
+            cols = slice(start, start + width)
+            nc.vector.tensor_tensor(out_sb[:, cols], banks[i][:], bias_sb[:, cols], ADD)
+            nc.sync.dma_start(out[0][:, cols], out_sb[:, cols])
+
+        for g, t in ((0, 0), (0, 1), (0, 2), (0, 3), (1, 0), (1, 1)):
+            gather(g, t, 0, HALF)
+            gather(g, t, HALF, HALF)
+            if (g, t) == (0, 3):
+                interleave(0, 0, HALF)
+                interleave(0, HALF, HALF)
+        for g in range(PASSES):
+            nc.scalar.copy(q_grouped[:, g], q_raw[:, g].rearrange("p t q -> p q t"))
+
+        gather(1, 2, 0, 512)
+        gather(1, 3, 0, 256)
+        interleave(1, 0, 256)
+        gather(1, 3, 256, 256)
+        interleave(1, 256, 256)
+        gather(1, 2, 512, 512)
+        gather(1, 3, 512, 256)
+        interleave(1, 512, 256)
+        gather(1, 3, 768, 128)
+        interleave(1, 768, 128)
+        gather(1, 3, 896, 128)
+        interleave(1, 896, 128)
+
+        nc.vector.quantize_mx(
+            out=q_codes[:].bitcast(FP8X4),
+            scales=q_scales[:],
+            in_=q_grouped[:].rearrange("p g q t -> p (g q t)"),
+        )
+        quantise(0, 0, N)
+        for i in range(len(PIECES)):
+            multiply(0, i)
+        for i, (start, width) in enumerate(PIECES):
+            quantise(1, start, width)
+            multiply(1, i)
+            if i >= 2:
+                finish(i - 2)
+        finish(2)
+        finish(3)

@@ -18,7 +18,7 @@ PACK = 4
 PASSES = D // (P * PACK)
 LIST = 16
 HALF = N // 2
-RUN = N // P
+RUN = HALF // P
 
 PIECES = [(0, 512), (512, 256), (768, 128), (896, 128)]
 
@@ -33,7 +33,7 @@ def tile_attend_pq_lin_bias_kernel(tc, qT, cb, norm, bias, offs, offs2, out):
         tc.psum_pool(name="psum", bufs=1) as psum,
     ):
         lists = [keep.tile([P, N // LIST], U16, name=f"list{g}") for g in range(PASSES)]
-        norm_runs = keep.tile([P, RUN], F32, name="norm_runs")
+        norm_runs = [keep.tile([P, RUN], F32, name=f"norm_runs{a}") for a in range(2)]
         identity = keep.tile([P, P], F32, name="identity")
         norm_sb = keep.tile([P, N], F32, name="norm_sb")
         bias_sb = keep.tile([P, N], F32, name="bias_sb")
@@ -48,11 +48,13 @@ def tile_attend_pq_lin_bias_kernel(tc, qT, cb, norm, bias, offs, offs2, out):
         k_scales = [keep.tile([P, N], U8, name=f"k_scales{g}", align_bytes=64) for g in range(PASSES)]
         out_sb = keep.tile([P, N], F32, name="out_sb")
         banks = [psum.tile([P, width], F32, name=f"bank{i}") for i, (start, width) in enumerate(PIECES)]
-        spread = [psum.tile([P, PACK, P], F32, name=f"spread{e}") for e in range(RUN // PACK)]
+        spread = [psum.tile([P, RUN, P], F32, name=f"spread{a}") for a in range(2)]
 
-        nc.scalar.dma_start(norm_runs[:], norm[0].rearrange("(p j) -> p j", j=RUN))
+        for a in range(2):
+            nc.scalar.dma_start(norm_runs[a][:], norm[0, a * HALF : (a + 1) * HALF].rearrange("(p j) -> p j", j=RUN))
+        nc.sync.dma_start(planes[0][0][:], cb_planes[0, 0])
         nc.sync.dma_start(lists[0][:], offs)
-        for t in range(PACK):
+        for t in range(1, PACK):
             nc.sync.dma_start(planes[0][t][:], cb_planes[0, t])
         nc.sync.dma_start(lists[1][:], offs2)
         nc.sync.dma_start(planes[1][0][:], cb_planes[1, 0])
@@ -63,14 +65,14 @@ def tile_attend_pq_lin_bias_kernel(tc, qT, cb, norm, bias, offs, offs2, out):
         nc.sync.dma_start(bias_sb[:], bias)
 
         make_identity(nc, identity[:])
-        for j in range(RUN):
-            nc.tensor.transpose(
-                spread[j // PACK][:, j % PACK, :], norm_runs[:, j : j + 1].to_broadcast([P, P]), identity[:]
-            )
-        norm_view = norm_sb[:].rearrange("p (n e j) -> p e n j", e=RUN // PACK, j=PACK)
-        for part in (slice(0, P // 2), slice(P // 2, P)):
-            for e, copy in ((0, nc.vector.tensor_copy), (1, nc.scalar.copy)):
-                copy(norm_view[:, e, part, :], spread[e][:, :, part].rearrange("p j n -> p n j"))
+        for a in range(2):
+            for j in range(RUN):
+                nc.tensor.transpose(
+                    spread[a][:, j, :], norm_runs[a][:, j : j + 1].to_broadcast([P, P]), identity[:]
+                )
+            norm_view = norm_sb[:, a * HALF : (a + 1) * HALF].rearrange("p (n j) -> p n j", j=RUN)
+            for part, copy in ((slice(0, P // 2), nc.vector.tensor_copy), (slice(P // 2, P), nc.scalar.copy)):
+                copy(norm_view[:, part, :], spread[a][:, :, part].rearrange("p j n -> p n j"))
 
         def gather(g, t, start, width):
             cols = slice(start, start + width)
@@ -83,6 +85,10 @@ def tile_attend_pq_lin_bias_kernel(tc, qT, cb, norm, bias, offs, offs2, out):
                 k_grouped[g][:, cols, :].rearrange("p (c i) t -> p c t i", i=4),
                 k_raw[g][:, :, cols].rearrange("p t (c i) -> p c t i", i=4),
             )
+
+        def interleave_pair(copy, g, t, start, width):
+            cols = slice(start, start + width)
+            copy(k_grouped[g][:, cols, t : t + 2], k_raw[g][:, t : t + 2, cols].rearrange("p t c -> p c t"))
 
         def quantise(g, start, width):
             cols = slice(start, start + width)
@@ -118,34 +124,40 @@ def tile_attend_pq_lin_bias_kernel(tc, qT, cb, norm, bias, offs, offs2, out):
             if (g, t) == (0, 3):
                 interleave(0, 0, HALF)
                 interleave(0, HALF, HALF)
+        interleave_pair(nc.scalar.copy, 1, 0, 0, HALF)
+        interleave_pair(nc.scalar.copy, 1, 0, HALF, HALF)
         for g in range(PASSES):
             nc.scalar.copy(q_grouped[:, g], q_raw[:, g].rearrange("p t q -> p q t"))
 
         gather(1, 2, 0, 512)
+        quantise(0, 0, N)
         gather(1, 3, 0, 256)
-        interleave(1, 0, 256)
+        interleave_pair(nc.scalar.copy, 1, 2, 0, 256)
         gather(1, 3, 256, 256)
-        interleave(1, 256, 256)
-        gather(1, 2, 512, 512)
-        gather(1, 3, 512, 256)
-        interleave(1, 512, 256)
-        gather(1, 3, 768, 128)
-        interleave(1, 768, 128)
-        gather(1, 3, 896, 128)
-        interleave(1, 896, 128)
-
+        interleave_pair(nc.scalar.copy, 1, 2, 256, 256)
         nc.vector.quantize_mx(
             out=q_codes[:].bitcast(FP8X4),
             scales=q_scales[:],
             in_=q_grouped[:].rearrange("p g q t -> p (g q t)"),
         )
-        quantise(0, 0, N)
+        gather(1, 2, 512, 512)
         for i in range(len(PIECES)):
             multiply(0, i)
-        for i, (start, width) in enumerate(PIECES):
-            quantise(1, start, width)
-            multiply(1, i)
-            if i >= 2:
-                finish(i - 2)
+        quantise(1, *PIECES[0])
+        multiply(1, 0)
+        gather(1, 3, 512, 256)
+        interleave_pair(nc.scalar.copy, 1, 2, 512, 256)
+        finish(0)
+        gather(1, 3, 768, 128)
+        interleave_pair(nc.scalar.copy, 1, 2, 768, 128)
+        gather(1, 3, 896, 128)
+        quantise(1, *PIECES[1])
+        multiply(1, 1)
+        interleave_pair(nc.vector.tensor_copy, 1, 2, 896, 128)
+        quantise(1, *PIECES[2])
+        multiply(1, 2)
+        finish(1)
+        quantise(1, *PIECES[3])
+        multiply(1, 3)
         finish(2)
         finish(3)

@@ -18,7 +18,7 @@ PACK = 4
 PASSES = D // (P * PACK)
 LIST = 16
 HALF = N // 2
-RUN = HALF // P
+RUN = N // P
 
 PIECES = [(0, 512), (512, 256), (768, 128), (896, 128)]
 
@@ -33,7 +33,7 @@ def tile_attend_pq_lin_bias_kernel(tc, qT, cb, norm, bias, offs, offs2, out):
         tc.psum_pool(name="psum", bufs=1) as psum,
     ):
         lists = [keep.tile([P, N // LIST], U16, name=f"list{g}") for g in range(PASSES)]
-        norm_runs = [keep.tile([P, RUN], F32, name=f"norm_runs{a}") for a in range(2)]
+        norm_runs = keep.tile([P, RUN], F32, name="norm_runs")
         identity = keep.tile([P, P], F32, name="identity")
         norm_sb = keep.tile([P, N], F32, name="norm_sb")
         bias_sb = keep.tile([P, N], F32, name="bias_sb")
@@ -48,10 +48,9 @@ def tile_attend_pq_lin_bias_kernel(tc, qT, cb, norm, bias, offs, offs2, out):
         k_scales = [keep.tile([P, N], U8, name=f"k_scales{g}", align_bytes=64) for g in range(PASSES)]
         out_sb = keep.tile([P, N], F32, name="out_sb")
         banks = [psum.tile([P, width], F32, name=f"bank{i}") for i, (start, width) in enumerate(PIECES)]
-        spread = [psum.tile([P, RUN, P], F32, name=f"spread{a}") for a in range(2)]
+        spread = [psum.tile([P, PACK, P], F32, name=f"spread{e}") for e in range(RUN // PACK)]
 
-        for a in range(2):
-            nc.scalar.dma_start(norm_runs[a][:], norm[0, a * HALF : (a + 1) * HALF].rearrange("(p j) -> p j", j=RUN))
+        nc.sync.dma_start(norm_runs[:], norm[0].rearrange("(p j) -> p j", j=RUN))
         nc.sync.dma_start(planes[0][0][:], cb_planes[0, 0])
         nc.sync.dma_start(lists[0][:], offs)
         for t in range(1, PACK):
@@ -65,14 +64,14 @@ def tile_attend_pq_lin_bias_kernel(tc, qT, cb, norm, bias, offs, offs2, out):
         nc.sync.dma_start(bias_sb[:], bias)
 
         make_identity(nc, identity[:])
-        for a in range(2):
-            for j in range(RUN):
-                nc.tensor.transpose(
-                    spread[a][:, j, :], norm_runs[a][:, j : j + 1].to_broadcast([P, P]), identity[:]
-                )
-            norm_view = norm_sb[:, a * HALF : (a + 1) * HALF].rearrange("p (n j) -> p n j", j=RUN)
-            for part, copy in ((slice(0, P // 2), nc.vector.tensor_copy), (slice(P // 2, P), nc.scalar.copy)):
-                copy(norm_view[:, part, :], spread[a][:, :, part].rearrange("p j n -> p n j"))
+        for j in range(RUN):
+            nc.tensor.transpose(
+                spread[j // PACK][:, j % PACK, :], norm_runs[:, j : j + 1].to_broadcast([P, P]), identity[:]
+            )
+        norm_view = norm_sb[:].rearrange("p (n e j) -> p e n j", e=RUN // PACK, j=PACK)
+        for part in (slice(0, P // 2), slice(P // 2, P)):
+            for e, copy in ((0, nc.vector.tensor_copy), (1, nc.scalar.copy)):
+                copy(norm_view[:, e, part, :], spread[e][:, :, part].rearrange("p j n -> p n j"))
 
         def gather(g, t, start, width):
             cols = slice(start, start + width)

@@ -35,16 +35,16 @@ def tile_attend_pq_lin_bias_kernel(tc, qT, cb, norm, bias, offs, offs2, out):
         lists = [keep.tile([P, N // LIST], U16, name=f"list{g}") for g in range(PASSES)]
         norm_runs = keep.tile([P, RUN], F32, name="norm_runs")
         identity = keep.tile([P, P], F32, name="identity")
-        norm_sb = keep.tile([P, N], F32, name="norm_sb")
+        norms = [keep.tile([P, HALF], F32, name=f"norm{a}", align_bytes=64) for a in range(2)]
         bias_sb = keep.tile([P, N], F32, name="bias_sb")
-        planes = [[keep.tile([P, C], F32, name=f"plane{g}{t}") for t in range(PACK)] for g in range(PASSES)]
+        planes = [
+            [keep.tile([P, C], F32, name=f"plane{g}{t}", align_bytes=64) for t in range(PACK)] for g in range(PASSES)
+        ]
         q_raw = keep.tile([P, PASSES, PACK, NQ], F32, name="q_raw")
         q_grouped = keep.tile([P, PASSES, NQ, PACK], BF16, name="q_grouped", align_bytes=64)
-        q_codes = keep.tile([P, PASSES * NQ], U32, name="q_codes", align_bytes=64)
         q_scales = keep.tile([P, PASSES * NQ], U8, name="q_scales", align_bytes=64)
-        k_raw = [keep.tile([P, PACK, N], F32, name=f"k_raw{g}") for g in range(PASSES)]
+        k_raw = [[keep.tile([P, PACK, HALF], F32, name=f"k_raw{g}{h}") for h in range(2)] for g in range(PASSES)]
         k_grouped = [keep.tile([P, N, PACK], BF16, name=f"k_grouped{g}", align_bytes=64) for g in range(PASSES)]
-        k_codes = [keep.tile([P, N], U32, name=f"k_codes{g}", align_bytes=64) for g in range(PASSES)]
         k_scales = [keep.tile([P, N], U8, name=f"k_scales{g}", align_bytes=64) for g in range(PASSES)]
         out_sb = keep.tile([P, N], F32, name="out_sb")
         banks = [psum.tile([P, width], F32, name=f"bank{i}") for i, (start, width) in enumerate(PIECES)]
@@ -65,34 +65,38 @@ def tile_attend_pq_lin_bias_kernel(tc, qT, cb, norm, bias, offs, offs2, out):
 
         make_identity(nc, identity[:])
         for j in range(RUN):
-            nc.tensor.transpose(
-                spread[j // PACK][:, j % PACK, :], norm_runs[:, j : j + 1].to_broadcast([P, P]), identity[:]
-            )
-        norm_view = norm_sb[:].rearrange("p (n e j) -> p e n j", e=RUN // PACK, j=PACK)
-        for part in (slice(0, P // 2), slice(P // 2, P)):
+            column = norm_runs[:, j : j + 1]
+            nc.tensor.transpose(spread[j // PACK][:, j % PACK, :], column.to_broadcast([P, P]), identity[:])
+        for half in range(2):
+            runs = norms[half][:].rearrange("p (n e j) -> p e n j", e=RUN // PACK, j=PACK)
+            part = slice(half * P // 2, (half + 1) * P // 2)
             for e, copy in ((0, nc.vector.tensor_copy), (1, nc.scalar.copy)):
-                copy(norm_view[:, e, part, :], spread[e][:, :, part].rearrange("p j n -> p n j"))
+                copy(runs[:, e], spread[e][:, :, part].rearrange("p j n -> p n j"))
 
         def gather(g, t, start, width):
-            cols = slice(start, start + width)
             entries = lists[g][:, start // LIST : (start + width) // LIST]
-            nc.vector.tensor_tensor(k_raw[g][:, t, cols], planes[g][t][:].indirect(entries), norm_sb[:, cols], MULT)
+            half, cols = start // HALF, slice(start % HALF, start % HALF + width)
+            nc.vector.tensor_tensor(
+                k_raw[g][half][:, t, cols], planes[g][t][:].indirect(entries), norms[half][:, cols], MULT
+            )
 
-        def interleave(g, start, width):
-            cols = slice(start, start + width)
+        def interleave(g, half):
             nc.scalar.copy(
-                k_grouped[g][:, cols, :].rearrange("p (c i) t -> p c t i", i=4),
-                k_raw[g][:, :, cols].rearrange("p t (c i) -> p c t i", i=4),
+                k_grouped[g][:, half * HALF : (half + 1) * HALF, :].rearrange("p (c i) t -> p c t i", i=4),
+                k_raw[g][half][:].rearrange("p t (c i) -> p c t i", i=4),
             )
 
         def interleave_pair(copy, g, t, start, width):
-            cols = slice(start, start + width)
-            copy(k_grouped[g][:, cols, t : t + 2], k_raw[g][:, t : t + 2, cols].rearrange("p t c -> p c t"))
+            half, cols = start // HALF, slice(start % HALF, start % HALF + width)
+            copy(
+                k_grouped[g][:, start : start + width, t : t + 2],
+                k_raw[g][half][:, t : t + 2, cols].rearrange("p t c -> p c t"),
+            )
 
-        def quantise(g, start, width):
+        def quantise(codes, g, start, width):
             cols = slice(start, start + width)
             nc.vector.quantize_mx(
-                out=k_codes[g][:, cols].bitcast(FP8X4),
+                out=codes[:, cols].bitcast(FP8X4),
                 scales=k_scales[g][:, cols],
                 in_=k_grouped[g][:, cols, :].rearrange("p c t -> p (c t)"),
             )
@@ -103,9 +107,9 @@ def tile_attend_pq_lin_bias_kernel(tc, qT, cb, norm, bias, offs, offs2, out):
             rows = slice(g * NQ, (g + 1) * NQ)
             nc.tensor.matmul_mx(
                 out=banks[i][:],
-                lhsT=q_codes[:, rows].bitcast(FP8X4),
+                lhsT=codes0[:, N + g * NQ : N + (g + 1) * NQ].bitcast(FP8X4),
                 lhsT_scale=q_scales[:, rows],
-                rhs=k_codes[g][:, cols].bitcast(FP8X4),
+                rhs=(codes0, codes1)[g][:, cols].bitcast(FP8X4),
                 rhs_scale=k_scales[g][:, cols],
                 start=(g == 0),
                 stop=(g == PASSES - 1),
@@ -118,45 +122,46 @@ def tile_attend_pq_lin_bias_kernel(tc, qT, cb, norm, bias, offs, offs2, out):
             nc.sync.dma_start(out[0][:, cols], out_sb[:, cols])
 
         for g, t in ((0, 0), (0, 1), (0, 2), (0, 3), (1, 0), (1, 1)):
-            gather(g, t, 0, HALF)
-            gather(g, t, HALF, HALF)
-            if (g, t) == (0, 3):
-                interleave(0, 0, HALF)
-                interleave(0, HALF, HALF)
-        interleave_pair(nc.scalar.copy, 1, 0, 0, HALF)
-        interleave_pair(nc.scalar.copy, 1, 0, HALF, HALF)
-        for g in range(PASSES):
-            nc.scalar.copy(q_grouped[:, g], q_raw[:, g].rearrange("p t q -> p q t"))
+            for half in range(2):
+                gather(g, t, half * HALF, HALF)
+            for half in range(2):
+                if (g, t) == (0, 3):
+                    interleave(0, half)
+                if (g, t) == (1, 1):
+                    interleave_pair(nc.scalar.copy, 1, 0, half * HALF, HALF)
+        for half in range(PASSES):
+            nc.scalar.copy(q_grouped[:, half], q_raw[:, half].rearrange("p t q -> p q t"))
 
-        gather(1, 2, 0, 512)
-        quantise(0, 0, N)
-        gather(1, 3, 0, 256)
-        interleave_pair(nc.scalar.copy, 1, 2, 0, 256)
-        gather(1, 3, 256, 256)
-        interleave_pair(nc.scalar.copy, 1, 2, 256, 256)
+        for start in (0, HALF):
+            gather(1, 2, start, HALF)
+        for start, width in ((0, 256), (256, 256)):
+            gather(1, 3, start, width)
+            interleave_pair(nc.scalar.copy, 1, 2, start, width)
+        codes0 = keep.tile([P, N + PASSES * NQ], U32, name="codes0", tag="norm0", align_bytes=64)
+        quantise(codes0, 0, 0, N)
+        gather(1, 3, 512, 256)
+        interleave_pair(nc.scalar.copy, 1, 2, 512, 256)
         nc.vector.quantize_mx(
-            out=q_codes[:].bitcast(FP8X4),
+            out=codes0[:, N:].bitcast(FP8X4),
             scales=q_scales[:],
             in_=q_grouped[:].rearrange("p g q t -> p (g q t)"),
         )
-        gather(1, 2, 512, 512)
-        for i in range(len(PIECES)):
-            multiply(0, i)
-        quantise(1, *PIECES[0])
-        multiply(1, 0)
-        gather(1, 3, 512, 256)
-        interleave_pair(nc.scalar.copy, 1, 2, 512, 256)
-        finish(0)
         gather(1, 3, 768, 128)
         interleave_pair(nc.scalar.copy, 1, 2, 768, 128)
         gather(1, 3, 896, 128)
-        quantise(1, *PIECES[1])
-        multiply(1, 1)
         interleave_pair(nc.vector.tensor_copy, 1, 2, 896, 128)
-        quantise(1, *PIECES[2])
+        codes1 = keep.tile([P, N], U32, name="codes1", tag="plane13", align_bytes=64)
+        for i in range(len(PIECES)):
+            multiply(0, i)
+        quantise(codes1, 1, *PIECES[0])
+        multiply(1, 0)
+        quantise(codes1, 1, *PIECES[1])
+        multiply(1, 1)
+        finish(0)
+        quantise(codes1, 1, *PIECES[2])
         multiply(1, 2)
         finish(1)
-        quantise(1, *PIECES[3])
+        quantise(codes1, 1, *PIECES[3])
         multiply(1, 3)
         finish(2)
         finish(3)

@@ -20,7 +20,7 @@ LIST = 16
 HALF = N // 2
 RUN = N // P
 
-PIECES = [(0, 512), (512, 256), (768, 128), (896, 128)]
+PIECES = [(0, 512), (512, 256), (768, 256)]
 
 
 def tile_attend_pq_lin_bias_kernel(tc, qT, cb, norm, bias, offs, offs2, out):
@@ -132,24 +132,23 @@ def tile_attend_pq_lin_bias_kernel(tc, qT, cb, norm, bias, offs, offs2, out):
         for half in range(PASSES):
             nc.scalar.copy(q_grouped[:, half], q_raw[:, half].rearrange("p t q -> p q t"))
 
-        for start in (0, HALF):
-            gather(1, 2, start, HALF)
-        for start, width in ((0, 256), (256, 256)):
-            gather(1, 3, start, width)
-            interleave_pair(nc.scalar.copy, 1, 2, start, width)
+        for half in range(2):
+            gather(1, 2, half * HALF, HALF)
+        gather(1, 3, *PIECES[0])
+        interleave_pair(nc.scalar.copy, 1, 2, *PIECES[0])
         codes0 = keep.tile([P, N + PASSES * NQ], U32, name="codes0", tag="norm0", align_bytes=64)
         quantise(codes0, 0, 0, N)
-        gather(1, 3, 512, 256)
-        interleave_pair(nc.scalar.copy, 1, 2, 512, 256)
+        gather(1, 3, *PIECES[1])
+        interleave_pair(nc.scalar.copy, 1, 2, *PIECES[1])
         nc.vector.quantize_mx(
             out=codes0[:, N:].bitcast(FP8X4),
             scales=q_scales[:],
             in_=q_grouped[:].rearrange("p g q t -> p (g q t)"),
         )
-        gather(1, 3, 768, 128)
+        gather(1, 3, *PIECES[2])
         interleave_pair(nc.scalar.copy, 1, 2, 768, 128)
-        gather(1, 3, 896, 128)
         interleave_pair(nc.vector.tensor_copy, 1, 2, 896, 128)
+
         codes1 = keep.tile([P, N], U32, name="codes1", tag="plane13", align_bytes=64)
         for i in range(len(PIECES)):
             multiply(0, i)
@@ -161,7 +160,4 @@ def tile_attend_pq_lin_bias_kernel(tc, qT, cb, norm, bias, offs, offs2, out):
         quantise(codes1, 1, *PIECES[2])
         multiply(1, 2)
         finish(1)
-        quantise(codes1, 1, *PIECES[3])
-        multiply(1, 3)
         finish(2)
-        finish(3)

import concourse.mybir as mybir
from concourse.masks import make_identity

NQ, D, N, C = 128, 1024, 1024, 2048
FLOPS = 2 * NQ * D * N

F32 = mybir.dt.float32
BF16 = mybir.dt.bfloat16
U32 = mybir.dt.uint32
U16 = mybir.dt.uint16
U8 = mybir.dt.uint8
FP8X4 = mybir.dt.float8_e4m3fn_x4
MULT = mybir.AluOpType.mult
ADD = mybir.AluOpType.add

P = 128
PACK = 4
PASSES = D // (P * PACK)
LIST = 16
HALF = N // 2
RUN = N // P

PIECES = [(0, 512), (512, 256), (768, 256)]


def tile_attend_pq_lin_bias_kernel(tc, qT, cb, norm, bias, offs, offs2, out):
    nc = tc.nc
    cb_planes = cb.rearrange("(g p t) c -> g t p c", g=PASSES, t=PACK)
    q_rows = qT[0].rearrange("(g p t) q -> p g t q", g=PASSES, t=PACK)

    with (
        tc.tile_pool(name="keep", bufs=1) as keep,
        tc.psum_pool(name="psum", bufs=1) as psum,
    ):
        lists = [keep.tile([P, N // LIST], U16, name=f"list{g}") for g in range(PASSES)]
        norm_runs = keep.tile([P, RUN], F32, name="norm_runs")
        identity = keep.tile([P, P], F32, name="identity")
        norms = [keep.tile([P, HALF], F32, name=f"norm{a}", align_bytes=64) for a in range(2)]
        bias_sb = keep.tile([P, N], F32, name="bias_sb")
        planes = [
            [keep.tile([P, C], F32, name=f"plane{g}{t}", align_bytes=64) for t in range(PACK)] for g in range(PASSES)
        ]
        q_raw = keep.tile([P, PASSES, PACK, NQ], F32, name="q_raw")
        q_grouped = keep.tile([P, PASSES, NQ, PACK], BF16, name="q_grouped", align_bytes=64)
        q_scales = keep.tile([P, PASSES * NQ], U8, name="q_scales", align_bytes=64)
        k_raw = [[keep.tile([P, PACK, HALF], F32, name=f"k_raw{g}{h}") for h in range(2)] for g in range(PASSES)]
        k_grouped = [keep.tile([P, N, PACK], BF16, name=f"k_grouped{g}", align_bytes=64) for g in range(PASSES)]
        k_scales = [keep.tile([P, N], U8, name=f"k_scales{g}", align_bytes=64) for g in range(PASSES)]
        out_sb = keep.tile([P, N], F32, name="out_sb")
        banks = [psum.tile([P, width], F32, name=f"bank{i}") for i, (start, width) in enumerate(PIECES)]
        spread = [psum.tile([P, PACK, P], F32, name=f"spread{e}") for e in range(RUN // PACK)]

        nc.sync.dma_start(norm_runs[:], norm[0].rearrange("(p j) -> p j", j=RUN))
        nc.sync.dma_start(planes[0][0][:], cb_planes[0, 0])
        nc.sync.dma_start(lists[0][:], offs)
        for t in range(1, PACK):
            nc.sync.dma_start(planes[0][t][:], cb_planes[0, t])
        nc.sync.dma_start(lists[1][:], offs2)
        nc.sync.dma_start(planes[1][0][:], cb_planes[1, 0])
        nc.sync.dma_start(planes[1][1][:], cb_planes[1, 1])
        nc.sync.dma_start(q_raw[:], q_rows)
        nc.sync.dma_start(planes[1][2][:], cb_planes[1, 2])
        nc.sync.dma_start(planes[1][3][:], cb_planes[1, 3])
        nc.sync.dma_start(bias_sb[:], bias)

        make_identity(nc, identity[:])
        for j in range(RUN):
            column = norm_runs[:, j : j + 1]
            nc.tensor.transpose(spread[j // PACK][:, j % PACK, :], column.to_broadcast([P, P]), identity[:])
        for half in range(2):
            runs = norms[half][:].rearrange("p (n e j) -> p e n j", e=RUN // PACK, j=PACK)
            part = slice(half * P // 2, (half + 1) * P // 2)
            for e, copy in ((0, nc.vector.tensor_copy), (1, nc.scalar.copy)):
                copy(runs[:, e], spread[e][:, :, part].rearrange("p j n -> p n j"))

        def gather(g, t, start, width):
            entries = lists[g][:, start // LIST : (start + width) // LIST]
            half, cols = start // HALF, slice(start % HALF, start % HALF + width)
            nc.vector.tensor_tensor(
                k_raw[g][half][:, t, cols], planes[g][t][:].indirect(entries), norms[half][:, cols], MULT
            )

        def interleave(g, half):
            nc.scalar.copy(
                k_grouped[g][:, half * HALF : (half + 1) * HALF, :].rearrange("p (c i) t -> p c t i", i=4),
                k_raw[g][half][:].rearrange("p t (c i) -> p c t i", i=4),
            )

        def interleave_pair(copy, g, t, start, width):
            half, cols = start // HALF, slice(start % HALF, start % HALF + width)
            copy(
                k_grouped[g][:, start : start + width, t : t + 2],
                k_raw[g][half][:, t : t + 2, cols].rearrange("p t c -> p c t"),
            )

        def quantise(codes, g, start, width):
            cols = slice(start, start + width)
            nc.vector.quantize_mx(
                out=codes[:, cols].bitcast(FP8X4),
                scales=k_scales[g][:, cols],
                in_=k_grouped[g][:, cols, :].rearrange("p c t -> p (c t)"),
            )

        def multiply(g, i):
            start, width = PIECES[i]
            cols = slice(start, start + width)
            rows = slice(g * NQ, (g + 1) * NQ)
            nc.tensor.matmul_mx(
                out=banks[i][:],
                lhsT=codes0[:, N + g * NQ : N + (g + 1) * NQ].bitcast(FP8X4),
                lhsT_scale=q_scales[:, rows],
                rhs=(codes0, codes1)[g][:, cols].bitcast(FP8X4),
                rhs_scale=k_scales[g][:, cols],
                start=(g == 0),
                stop=(g == PASSES - 1),
            )

        def finish(i):
            start, width = PIECES[i]
            cols = slice(start, start + width)
            nc.vector.tensor_tensor(out_sb[:, cols], banks[i][:], bias_sb[:, cols], ADD)
            nc.sync.dma_start(out[0][:, cols], out_sb[:, cols])

        for g, t in ((0, 0), (0, 1), (0, 2), (0, 3), (1, 0), (1, 1)):
            for half in range(2):
                gather(g, t, half * HALF, HALF)
            for half in range(2):
                if (g, t) == (0, 3):
                    interleave(0, half)
                if (g, t) == (1, 1):
                    interleave_pair(nc.scalar.copy, 1, 0, half * HALF, HALF)
        for half in range(PASSES):
            nc.scalar.copy(q_grouped[:, half], q_raw[:, half].rearrange("p t q -> p q t"))

        for half in range(2):
            gather(1, 2, half * HALF, HALF)
        gather(1, 3, *PIECES[0])
        interleave_pair(nc.scalar.copy, 1, 2, *PIECES[0])
        codes0 = keep.tile([P, N + PASSES * NQ], U32, name="codes0", tag="norm0", align_bytes=64)
        quantise(codes0, 0, 0, N)
        gather(1, 3, *PIECES[1])
        interleave_pair(nc.scalar.copy, 1, 2, *PIECES[1])
        nc.vector.quantize_mx(
            out=codes0[:, N:].bitcast(FP8X4),
            scales=q_scales[:],
            in_=q_grouped[:].rearrange("p g q t -> p (g q t)"),
        )
        gather(1, 3, *PIECES[2])
        interleave_pair(nc.scalar.copy, 1, 2, 768, 128)
        interleave_pair(nc.vector.tensor_copy, 1, 2, 896, 128)

        codes1 = keep.tile([P, N], U32, name="codes1", tag="plane13", align_bytes=64)
        for i in range(len(PIECES)):
            multiply(0, i)
        quantise(codes1, 1, *PIECES[0])
        multiply(1, 0)
        quantise(codes1, 1, *PIECES[1])
        multiply(1, 1)
        finish(0)
        quantise(codes1, 1, *PIECES[2])
        multiply(1, 2)
        finish(1)
        finish(2)
